import numpy as np
import ml_dtypes


def mxq(x, axis, fmt="e4m3"):
    dtype, down = {"e4m3": (ml_dtypes.float8_e4m3fn, 7), "e5m2": (ml_dtypes.float8_e5m2, 14)}[fmt]
    v = np.moveaxis(np.asarray(x, np.float32).astype(ml_dtypes.bfloat16).astype(np.float64), axis, -1)
    blocks = v.reshape(v.shape[:-1] + (-1, 32))
    amax = np.abs(blocks).max(-1, keepdims=True)
    byte = np.maximum(np.where(amax > 0, np.frexp(amax)[1] - 1 + 127, 0) - down, 1)
    scale = np.exp2(byte - 127.0)
    codes = (blocks / scale).astype(np.float32).astype(dtype).astype(np.float64)
    return np.moveaxis((codes * scale).reshape(v.shape), -1, axis)


WIDE = False


def mx_kscale(k):
    if not WIDE:
        return np.ones(k)
    levels = np.array([30, -30])
    if k % 512:
        return np.exp2(np.random.permutation(np.resize(levels, k // 32))).repeat(32)
    a = np.empty((k // 512, 16))
    for p in range(k // 512):
        a[p, :8] = np.random.permutation(np.resize(levels, 8))
        for g in range(8):
            far = levels[np.abs(levels - a[p, g]) >= 10]
            a[p, g + 8] = far[np.random.randint(len(far))]
    return np.exp2(a.ravel()).repeat(32)


def f64(x):
    return np.asarray(x).astype(np.float64)


def striped(idx):
    return np.tile(np.asarray(idx).reshape(-1, 16).T, (8, 1)).astype(np.uint16)


def unstriped(offs):
    return offs[:16].T.reshape(-1).astype(np.int64)


E2M1 = np.array([0.0, 0.5, 1.0, 1.5, 2.0, 3.0, 4.0, 6.0, -0.0, -0.5, -1.0, -1.5, -2.0, -3.0, -4.0, -6.0])


def pack_weight(w, fmt):
    k, n = w.shape
    w = f64(np.asarray(w, np.float32).astype(ml_dtypes.bfloat16)).reshape(k // 32, 32, n)
    amax = np.abs(w).max(1)
    if fmt in ("e4m3", "e5m2"):
        byte = np.frexp(amax)[1] - 1 + 127 - (7 if fmt == "e4m3" else 14)
    else:
        mant, ex = np.frexp(amax / 6.0)
        byte = np.where(mant > 0.5, ex, ex - 1) + 127
    byte = np.clip(np.where(amax > 0, byte, 1), 1, 254)
    scaled = (w * np.exp2(127.0 - byte)[:, None, :]).reshape(k, n).astype(np.float32)
    by_word = np.ascontiguousarray(scaled.reshape(k // 512, 128, 4, n).transpose(0, 1, 3, 2))
    if fmt in ("e4m3", "e5m2"):
        words = by_word.astype(ml_dtypes.float8_e4m3fn if fmt == "e4m3" else ml_dtypes.float8_e5m2).view(np.uint8)
    else:
        c = by_word.astype(ml_dtypes.float4_e2m1fn).view(np.uint8) & 0xF
        words = (c[..., 0::2] | (c[..., 1::2] << 4)).reshape(k // 512, 128, 2 * n)
    return np.ascontiguousarray(words), np.ascontiguousarray(byte.astype(np.uint8).reshape(k // 512, 16, n))


def unpack_weight(words, scales, fmt):
    g, _, n = scales.shape
    words = np.ascontiguousarray(words).reshape(g, 128, n, -1)
    if fmt in ("e4m3", "e5m2"):
        vals = words.view(ml_dtypes.float8_e4m3fn if fmt == "e4m3" else ml_dtypes.float8_e5m2).astype(np.float64)
    else:
        nib = np.empty((g, 128, n, 4), np.uint8)
        nib[..., 0::2] = words & 0xF
        nib[..., 1::2] = words >> 4
        vals = E2M1[nib]
    vals = vals * np.repeat(np.exp2(scales.astype(np.float64) - 127.0), 8, axis=1)[..., None]
    return vals.transpose(0, 1, 3, 2).reshape(g * 512, n)


K, T, J, R, F, Z, I, O, N, S, E = 512, 1024, 256, 512, 512, 1024, 256, 128, 256, 1024, 1024


def setup_inputs():
    n = np.random.standard_normal
    idx = np.random.permutation(T)[:J]
    idx2 = np.random.permutation(Z)[:J]
    idx3 = np.random.permutation(J)[:I]
    idx4 = np.random.permutation(I)[:O]
    idx5 = np.random.permutation(J)[:O]
    idx6 = np.random.permutation(S)[:N]
    idx7 = np.random.permutation(E)[:O]
    fk = mx_kscale(K)
    ff = mx_kscale(F)
    fr = mx_kscale(R)
    xtp = pack_weight(n((K, T)) / fk[:, None], "e4m3")
    xop = pack_weight(n((F, Z)) / ff[:, None], "e2m1")
    wp = pack_weight(n((K, R)) * 1 / np.sqrt(K) * fk[:, None] * fr, "e2m1")
    w2p = pack_weight(n((K, R)) * 1 / np.sqrt(K) * fk[:, None], "e5m2")
    w0p = pack_weight(n((F, R)) * 1 / np.sqrt(F) * ff[:, None], "e5m2")
    vsp = pack_weight(n((R, S)) * 1 / np.sqrt(R) / fr[:, None], "e5m2")
    return {
        "xt_words": xtp[0],
        "xt_scales": xtp[1],
        "xo_words": xop[0],
        "xo_scales": xop[1],
        "w_words": wp[0],
        "w_scales": wp[1],
        "w2_words": w2p[0],
        "w2_scales": w2p[1],
        "w0_words": w0p[0],
        "w0_scales": w0p[1],
        "vs_words": vsp[0],
        "vs_scales": vsp[1],
        "offs": striped(idx),
        "offs2": striped(idx2),
        "offs3": striped(idx3),
        "offs4": striped(idx4),
        "offs5": striped(idx5),
        "offs6": striped(idx6),
        "offs7": striped(idx7),
    }


def reference(xt_words, xt_scales, xo_words, xo_scales, w_words, w_scales, w2_words, w2_scales, w0_words, w0_scales, vs_words, vs_scales, offs, offs2, offs3, offs4, offs5, offs6, offs7):
    idx = unstriped(offs)
    idx2 = unstriped(offs2)
    idx3 = unstriped(offs3)
    idx4 = unstriped(offs4)
    idx5 = unstriped(offs5)
    idx6 = unstriped(offs6)
    idx7 = unstriped(offs7)
    xtu = unpack_weight(xt_words, xt_scales, "e4m3")
    xou = unpack_weight(xo_words, xo_scales, "e2m1")
    wu = unpack_weight(w_words, w_scales, "e2m1")
    w2u = unpack_weight(w2_words, w2_scales, "e5m2")
    w0u = unpack_weight(w0_words, w0_scales, "e5m2")
    vsu = unpack_weight(vs_words, vs_scales, "e5m2")
    xtidxg = xtu[:, idx]
    a = wu.T @ xtidxg
    xoidx2g = xou[:, idx2]
    b = w2u.T @ xtidxg + w0u.T @ xoidx2g
    lb = b[:, 0:1]
    h1 = a[:, idx3] * lb
    lh = h1[:, 0:1]
    hid = np.abs(h1[:, idx4] - b[:, idx5] * lh)
    vsidx6g = vsu[:, idx6]
    hidq = mxq(hid, 0, "e4m3")
    p = vsidx6g.T @ hidq
    y = np.zeros((N, E))
    y[:, idx7] = p
    return y

from contextlib import ExitStack

import concourse.mybir as mybir

F32 = mybir.dt.float32
BF16 = mybir.dt.bfloat16
I32 = mybir.dt.int32
U32 = mybir.dt.uint32
U16 = mybir.dt.uint16
U8 = mybir.dt.uint8
E4M3 = mybir.dt.float8_e4m3fn_x4
E5M2 = mybir.dt.float8_e5m2_x4
E2M1 = mybir.dt.float4_e2m1fn_x4
ACT = mybir.ActivationFunctionType
ALU = mybir.AluOpType

P = 128
PACK = 4
QUADS = 4
K, T, J, R, F, Z, I, O, N, S, E = 512, 1024, 256, 512, 512, 1024, 256, 128, 256, 1024, 1024

FLOPS = 2 * (K * R * J * 2 + F * R * J + R * N * O)


def tile_list_pickleads_leaned_store_scattered_kernel(
    tc, xt_words, xt_scales, xo_words, xo_scales, w_words, w_scales, w2_words, w2_scales,
    w0_words, w0_scales, vs_words, vs_scales, offs, offs2, offs3, offs4, offs5, offs6, offs7, out,
):
    nc = tc.nc
    with ExitStack() as ctx:
        sb = ctx.enter_context(tc.tile_pool(name="sb", bufs=1))
        ps = ctx.enter_context(tc.psum_pool(name="ps", bufs=1))

        def tile(name, cols, dtype):
            return sb.tile([P, cols], dtype, name=name, align_bytes=64)

        def load_list(name, src):
            dst = sb.tile([P, src.shape[1]], U16, name=name)
            nc.sync.dma_start(dst[:], src)
            return dst

        def load_words(name, src, cols, dtype):
            dst = tile(name, cols, dtype)
            rows = src[0]
            if len(rows.shape) == 3:
                rows = rows.rearrange("p n t -> p (n t)")
            nc.sync.dma_start(dst[:].bitcast(I32), rows.bitcast(I32))
            return dst

        def zeroed_scales(name, cols):
            dst = tile(name, cols, U8)
            nc.vector.memset(dst[:].bitcast(I32), 0)
            return dst

        def load_scales(queue, dst, src):
            for q in range(QUADS):
                queue.dma_start(dst[32 * q : 32 * q + 4, :].bitcast(I32), src[0, 4 * q : 4 * q + 4, :].bitcast(I32))

        def gather(name, window, lst, dtype):
            dst = tile(name, 16 * lst.shape[1], dtype)
            nc.vector.tensor_copy(dst[:], window[:].indirect(lst[:]))
            return dst

        def deal(copy, name, src, dtype):
            dst = tile(name, R, dtype)
            copy(dst[:].rearrange("p (t m) -> p m t", t=PACK), src[:].rearrange("p (m t) -> p m t", t=PACK))
            return dst

        xt_s = zeroed_scales("xt_s", T)
        xo_s = zeroed_scales("xo_s", Z)
        w2_s = zeroed_scales("w2_s", R)
        w0_s = zeroed_scales("w0_s", R)
        w_s = zeroed_scales("w_s", R)
        vs_s = zeroed_scales("vs_s", S)
        pages = [sb.tile([P, E], F32, name="page%d" % h) for h in range(N // P)]
        for page in pages:
            nc.vector.memset(page[:], 0.0)

        l1 = load_list("l1", offs)
        xt_w = load_words("xt_w", xt_words, T, U32)
        load_scales(nc.scalar, xt_s, xt_scales)
        l2 = load_list("l2", offs2)
        w2_w = load_words("w2_w", w2_words, R, U32)
        load_scales(nc.scalar, xo_s, xo_scales)
        xo_w = load_words("xo_w", xo_words, Z, U16)
        w0_w = load_words("w0_w", w0_words, R, U32)
        w_w = load_words("w_w", w_words, R, U16)
        load_scales(nc.gpsimd, w_s, w_scales)
        load_scales(nc.sync, w2_s, w2_scales)
        load_scales(nc.sync, w0_s, w0_scales)
        l3 = load_list("l3", offs3)
        vs_w = load_words("vs_w", vs_words, S, U32)
        l6 = load_list("l6", offs6)
        load_scales(nc.sync, vs_s, vs_scales)
        l5 = load_list("l5", offs5)
        l4 = load_list("l4", offs4)
        l7 = load_list("l7", offs7)

        xt_gw = gather("xt_gw", xt_w, l1, U32)
        xt_gs = gather("xt_gs", xt_s, l1, U8)
        w2_dw = deal(nc.scalar.copy, "w2_dw", w2_w, U32)
        xo_gw = gather("xo_gw", xo_w, l2, U16)
        xo_gs = gather("xo_gs", xo_s, l2, U8)
        w0_dw = deal(nc.scalar.copy, "w0_dw", w0_w, U32)
        w_dw = deal(nc.scalar.copy, "w_dw", w_w, U16)
        w2_ds = deal(nc.vector.tensor_copy, "w2_ds", w2_s, U8)
        w0_ds = deal(nc.vector.tensor_copy, "w0_ds", w0_s, U8)
        w_ds = deal(nc.vector.tensor_copy, "w_ds", w_s, U8)

        a_ps, b_ps = [], []
        for t in range(PACK):
            cols = slice(t * P, (t + 1) * P)
            b_t = ps.tile([P, J], F32, name="b_ps%d" % t, tag="bank_b%d" % t)
            nc.tensor.matmul_mx(out=b_t[:], lhsT=w2_dw[:, cols].bitcast(E5M2), lhsT_scale=w2_ds[:, cols],
                                rhs=xt_gw[:].bitcast(E4M3), rhs_scale=xt_gs[:], start=True, stop=False)
            nc.tensor.matmul_mx(out=b_t[:], lhsT=w0_dw[:, cols].bitcast(E5M2), lhsT_scale=w0_ds[:, cols],
                                rhs=xo_gw[:].bitcast(E2M1), rhs_scale=xo_gs[:], start=False, stop=True)
            a_t = ps.tile([P, J], F32, name="a_ps%d" % t, tag="bank_a%d" % t)
            nc.tensor.matmul_mx(out=a_t[:], lhsT=w_dw[:, cols].bitcast(E2M1), lhsT_scale=w_ds[:, cols],
                                rhs=xt_gw[:].bitcast(E4M3), rhs_scale=xt_gs[:], start=True, stop=True)
            a_ps.append(a_t)
            b_ps.append(b_t)

        a_sb = [sb.tile([P, 2 * J], F32, name="a_sb%d" % t) for t in range(PACK)]
        b_sb = [sb.tile([P, J], F32, name="b_sb%d" % t) for t in range(PACK)]
        h1 = [sb.tile([P, I], F32, name="h1_%d" % t) for t in range(PACK)]
        bl = [sb.tile([P, O], F32, name="bl%d" % t) for t in range(PACK)]
        diff = sb.tile([P, PACK, O], F32, name="diff")

        def unload(t):
            nc.vector.tensor_copy(b_sb[t][:], b_ps[t][:])
            if t == 0:
                nc.scalar.copy(a_sb[t][:, 0:J], a_ps[t][:])
            else:
                nc.vector.tensor_copy(a_sb[t][:, 0:J], a_ps[t][:])

        def pick(t):
            nc.scalar.activation(out=h1[t][:], in_=a_sb[t][:].indirect(l3[:]), func=ACT.Copy, scale=b_sb[t][:, 0:1])

        def lean(t):
            nc.scalar.activation(out=bl[t][:], in_=b_sb[t][:].indirect(l5[:]), func=ACT.Copy, scale=h1[t][:, 0:1])

        def subtract(t):
            nc.vector.tensor_tensor(diff[:, t, :], h1[t][:].indirect(l4[:]), bl[t][:], ALU.subtract)

        for t in range(PACK):
            unload(t)
        pick(0)
        for t in range(1, PACK):
            pick(t)
            lean(t - 1)
        lean(PACK - 1)
        vs_gw = gather("vs_gw", vs_w, l6, U32)
        vs_gs = gather("vs_gs", vs_s, l6, U8)
        for t in range(PACK):
            subtract(t)

        hid = sb.tile([P, O, PACK], BF16, name="hid", align_bytes=64)
        woven = diff[:].rearrange("p t o -> p o t")
        half = O // 2
        nc.scalar.activation(out=hid[:, half:, :], in_=woven[:, half:, :], func=ACT.Abs)
        nc.vector.scalar_tensor_tensor(out=hid[:, :half, :], in0=woven[:, :half, :], scalar=-1.0,
                                       in1=woven[:, :half, :], op0=ALU.mult, op1=ALU.max)
        hid_w = tile("hid_w", O, U32)
        hid_s = tile("hid_s", O, U8)
        nc.vector.quantize_mx(out=hid_w[:].bitcast(E4M3), scales=hid_s[:], in_=hid[:].rearrange("p o t -> p (o t)"))

        for h, (copy, queue) in enumerate(((nc.vector.tensor_copy, nc.sync), (nc.scalar.copy, nc.scalar))):
            cols = slice(h * P, (h + 1) * P)
            p_ps = ps.tile([P, O], F32, name="p_ps%d" % h, tag="bank_a%d" % h)
            nc.tensor.matmul_mx(out=p_ps[:], lhsT=vs_gw[:, cols].bitcast(E5M2), lhsT_scale=vs_gs[:, cols],
                                rhs=hid_w[:].bitcast(E4M3), rhs_scale=hid_s[:], start=True, stop=True)
            p_sb = sb.tile([P, O], F32, name="p_sb%d" % h)
            copy(p_sb[:], p_ps[:])
            if h == 0:
                nc.vector.tensor_copy(pages[h][:].indirect(l7[:]), p_sb[:])
            else:
                nc.scalar.activation(out=pages[h][:].indirect(l7[:]), in_=p_sb[:], func=ACT.Copy)
            queue.dma_start(out[cols, :], pages[h][:])
